import numpy as np
import ml_dtypes


def mxq(x, axis, fmt="e4m3"):
    dtype, down = {"e4m3": (ml_dtypes.float8_e4m3fn, 7), "e5m2": (ml_dtypes.float8_e5m2, 14)}[fmt]
    v = np.moveaxis(np.asarray(x, np.float32).astype(ml_dtypes.bfloat16).astype(np.float64), axis, -1)
    blocks = v.reshape(v.shape[:-1] + (-1, 32))
    amax = np.abs(blocks).max(-1, keepdims=True)
    byte = np.maximum(np.where(amax > 0, np.frexp(amax)[1] - 1 + 127, 0) - down, 1)
    scale = np.exp2(byte - 127.0)
    codes = (blocks / scale).astype(np.float32).astype(dtype).astype(np.float64)
    return np.moveaxis((codes * scale).reshape(v.shape), -1, axis)


WIDE = False


def mx_kscale(k):
    if not WIDE:
        return np.ones(k)
    levels = np.array([10, -10, 5, -5, 0])
    if k % 512:
        return np.exp2(np.random.permutation(np.resize(levels, k // 32))).repeat(32)
    a = np.empty((k // 512, 16))
    for p in range(k // 512):
        a[p, :8] = np.random.permutation(np.resize(levels, 8))
        for g in range(8):
            far = levels[np.abs(levels - a[p, g]) >= 10]
            a[p, g + 8] = far[np.random.randint(len(far))]
    return np.exp2(a.ravel()).repeat(32)


def f64(x):
    return np.asarray(x).astype(np.float64)


def striped(idx):
    return np.tile(idx.reshape(-1, 16).T, (8, 1)).astype(np.uint16)


def unstriped(offs):
    return offs[:16].T.reshape(-1).astype(np.int64)


def relu(v):
    return np.maximum(v, 0.0)


K, T, D, S, V, N = 1536, 512, 8, 2048, 256, 256


def setup_inputs():
    n = np.random.standard_normal
    s = mx_kscale(K)[:, None]
    return {
        "xT": (n((K, T)) * s).astype(np.float32),
        "w": (n((K, N)) / np.sqrt(K) / s).astype(np.float32),
        "b": (0.3 * n((N, 1))).astype(np.float32),
        "gate": np.tile(np.random.uniform(0.2, 1.0, (D, 1, V)) / np.sqrt(D), (1, N, 1)).astype(np.float32),
        "pos1": striped(np.random.permutation(T)[:V]),
        "pos2": striped(np.random.permutation(T)[:V]),
        "pos3": striped(np.random.permutation(T)[:V]),
        "pos4": striped(np.random.permutation(T)[:V]),
        "pos5": striped(np.random.permutation(T)[:V]),
        "pos6": striped(np.random.permutation(T)[:V]),
        "pos7": striped(np.random.permutation(T)[:V]),
        "pos8": striped(np.random.permutation(T)[:V]),
    }


def reference(xT, w, b, gate, pos1, pos2, pos3, pos4, pos5, pos6, pos7, pos8):
    y = mxq(f64(w), 0, "e4m3").T @ mxq(f64(xT), 0, "e4m3")
    y = relu(y + f64(b))
    return sum(f64(gate[d]) * y[:, unstriped(p)] for d, p in enumerate((pos1, pos2, pos3, pos4, pos5, pos6, pos7, pos8)))

@@ -1,0 +1,221 @@
+from contextlib import ExitStack
+
+import concourse.mybir as mybir
+from concourse.masks import make_identity
+
+K, T, D, V, N = 1536, 512, 8, 256, 256
+FLOPS = 2 * K * T * N + 2 * D * V * N
+
+F32 = mybir.dt.float32
+BF16 = mybir.dt.bfloat16
+U32 = mybir.dt.uint32
+U16 = mybir.dt.uint16
+U8 = mybir.dt.uint8
+FP8X4 = mybir.dt.float8_e4m3fn_x4
+ADD = mybir.AluOpType.add
+MULT = mybir.AluOpType.mult
+MAX = mybir.AluOpType.max
+RELU = mybir.ActivationFunctionType.Relu
+
+P = 128
+PACK = 4
+K_PASS = P * PACK
+PASSES = K // K_PASS
+HALVES = N // P
+NODE_GROUPS = ((0, 256), (256, 384), (384, 512))
+TAIL_TURNS = 2
+
+
+def interleave(copy, grouped, raw, src0, dst0, width):
+    src = raw[:, :, src0 : src0 + width].rearrange("p j (c i) -> p c j i", i=4)
+    dst = grouped[:, dst0 : dst0 + width, :].rearrange("p (c i) j -> p c j i", i=4)
+    copy(dst, src)
+
+
+def quantize(nc, codes, scales, grouped, c0, c1):
+    nc.vector.quantize_mx(
+        out=codes[:, c0:c1].bitcast(FP8X4),
+        scales=scales[:, c0:c1],
+        in_=grouped[:, c0:c1, :].rearrange("p w j -> p (w j)"),
+    )
+
+
+def tile_picked_agg_lin_relu_sub_l_kernel(
+    tc, xT, w, b, gate, pos1, pos2, pos3, pos4, pos5, pos6, pos7, pos8, out
+):
+    nc = tc.nc
+    lists = (pos1, pos2, pos3, pos4, pos5, pos6, pos7, pos8)
+    on_vector = nc.vector.tensor_copy
+    on_scalar = nc.scalar.copy
+
+    with ExitStack() as ctx:
+        keep = ctx.enter_context(tc.tile_pool(name="keep", bufs=1))
+        psum = ctx.enter_context(tc.psum_pool(name="psum", bufs=1))
+
+        offsets = [keep.tile([P, V // 16], U16, name=f"offsets{d}") for d in range(D)]
+        bias = keep.tile([P, HALVES], F32, name="bias")
+        identity = keep.tile([P, P], F32, name="identity")
+        warm_in = keep.tile([P, 1], F32, name="warm_in")
+        warm_out = keep.tile([P, 1], F32, name="warm_out")
+
+        x_bf = [keep.tile([P, T, PACK], BF16, name=f"x_bf{c}", align_bytes=64) for c in range(PASSES)]
+        x_codes = [keep.tile([P, T], U32, name=f"x_codes{c}", align_bytes=64) for c in range(PASSES)]
+        x_scales = [keep.tile([P, T], U8, name=f"x_scales{c}", align_bytes=64) for c in range(PASSES)]
+        hc = [(h, c) for h in range(HALVES) for c in range(PASSES)]
+        w_raw = {(h, c): keep.tile([P, PACK, P], F32, name=f"w_raw{h}{c}") for h, c in hc}
+        w_bf = {(h, c): keep.tile([P, P, PACK], BF16, name=f"w_bf{h}{c}", align_bytes=64) for h, c in hc}
+        w_codes = {(h, c): keep.tile([P, P], U32, name=f"w_codes{h}{c}", align_bytes=64) for h, c in hc}
+        w_scales = {(h, c): keep.tile([P, P], U8, name=f"w_scales{h}{c}", align_bytes=64) for h, c in hc}
+        y = [keep.tile([P, T], F32, name=f"y{h}") for h in range(HALVES)]
+        result = [keep.tile([P, V], F32, name=f"result{h}") for h in range(HALVES)]
+
+        def load_x(c, t0, t1):
+            raw = keep.tile([P, PACK, t1 - t0], F32, name=f"x_raw{c}_{t0}")
+            rows = xT[c * K_PASS : (c + 1) * K_PASS, t0:t1]
+            nc.sync.dma_start(raw[:], rows.rearrange("(p j) t -> p j t", j=PACK))
+            return raw
+
+        def load_w(h, c):
+            rows = w[c * K_PASS : (c + 1) * K_PASS, h * P : (h + 1) * P]
+            nc.sync.dma_start(w_raw[h, c][:], rows.rearrange("(p j) m -> p j m", j=PACK))
+
+        gates = {}
+
+        def load_gate(h, d0, d1):
+            tile = keep.tile([P, d1 - d0, V], F32, name=f"gate{h}_{d0}")
+            nc.sync.dma_start(tile[:], gate[d0:d1, h * P : (h + 1) * P, :].rearrange("d m v -> m d v"))
+            for d in range(d0, d1):
+                gates[h, d] = tile[:, d - d0, :]
+
+        def load_list(d):
+            nc.sync.dma_start(offsets[d][:], lists[d])
+
+        def project(bank, h, c, t0, t1):
+            nc.tensor.matmul_mx(
+                out=bank[:, 0 : t1 - t0],
+                lhsT=w_codes[h, c][:].bitcast(FP8X4),
+                lhsT_scale=w_scales[h, c][:],
+                rhs=x_codes[c][:, t0:t1].bitcast(FP8X4),
+                rhs_scale=x_scales[c][:, t0:t1],
+                start=(c == 0),
+                stop=(c == PASSES - 1),
+            )
+
+        with nc.allow_non_contiguous_dma(reason="one bias value a partition"):
+            nc.scalar.dma_start(bias[:], b.rearrange("(h p) o -> p (h o)", p=P))
+        nc.vector.memset(warm_in[:], 0.0)
+        nc.scalar.activation(warm_out[:], warm_in[:], RELU)
+        make_identity(nc, identity[:])
+
+        x_raw = {}
+        x_raw[0] = load_x(0, 0, T)
+        load_w(0, 0)
+        x_raw[1] = load_x(1, 0, T)
+        load_w(0, 1)
+        load_w(0, 2)
+        last = [load_x(2, t0, t1) for t0, t1 in NODE_GROUPS]
+        load_list(0)
+        load_gate(0, 0, 1)
+        load_w(1, 0)
+        load_list(1)
+        load_gate(0, 1, 3)
+        load_w(1, 1)
+        load_w(1, 2)
+        load_list(2)
+        load_list(3)
+        load_gate(0, 3, 5)
+        load_list(4)
+        load_list(5)
+        load_gate(0, 5, 8)
+        load_list(6)
+        load_list(7)
+        load_gate(1, 0, 4)
+        load_gate(1, 4, 8)
+
+        banks = [psum.tile([P, T], F32, name=f"bank{g}") for g in range(len(NODE_GROUPS))]
+        for c in range(PASSES - 1):
+            interleave(on_scalar, x_bf[c], x_raw[c], 0, 0, 256)
+            interleave(on_vector, x_bf[c], x_raw[c], 256, 256, 256)
+            interleave(on_scalar, w_bf[0, c], w_raw[0, c], 0, 0, P)
+            quantize(nc, x_codes[c], x_scales[c], x_bf[c], 256, 512)
+            quantize(nc, x_codes[c], x_scales[c], x_bf[c], 0, 256)
+            quantize(nc, w_codes[0, c], w_scales[0, c], w_bf[0, c], 0, P)
+            for bank, (t0, t1) in zip(banks, NODE_GROUPS):
+                project(bank, 0, c, t0, t1)
+
+        c = PASSES - 1
+        interleave(on_scalar, w_bf[0, c], w_raw[0, c], 0, 0, P)
+        quantize(nc, w_codes[0, c], w_scales[0, c], w_bf[0, c], 0, P)
+        interleave(on_scalar, x_bf[c], last[0], 0, 0, 128)
+        interleave(on_vector, x_bf[c], last[0], 128, 128, 128)
+        interleave(on_vector, x_bf[c], last[1], 0, 256, 128)
+        quantize(nc, x_codes[c], x_scales[c], x_bf[c], 0, 256)
+        project(banks[0], 0, c, 0, 256)
+        interleave(on_scalar, x_bf[c], last[2], 0, 384, 64)
+        interleave(on_vector, x_bf[c], last[2], 64, 448, 64)
+        quantize(nc, x_codes[c], x_scales[c], x_bf[c], 256, 384)
+        project(banks[1], 0, c, 256, 384)
+        quantize(nc, x_codes[c], x_scales[c], x_bf[c], 384, 512)
+        project(banks[2], 0, c, 384, 512)
+        nc.scalar.activation(y[0][:, 0:256], banks[0][:, 0:256], RELU, bias=bias[:, 0:1])
+        nc.scalar.activation(y[0][:, 256:384], banks[1][:, 0:128], RELU, bias=bias[:, 0:1])
+        nc.vector.tensor_scalar(y[0][:, 384:512], banks[2][:, 0:128], bias[:, 0:1], 0.0, ADD, MAX)
+
+        products = {}
+
+        def gather(h, d):
+            products[h, d] = keep.tile([P, V], F32, name=f"product{h}_{d}")
+            nc.vector.tensor_tensor(products[h, d][:], y[h][:].indirect(offsets[d][:]), gates[h, d], MULT)
+
+        def add_turned(bank, h, d, turns):
+            for u in range(V // P):
+                nc.tensor.matmul(
+                    bank[:, u * P : (u + 1) * P],
+                    lhsT=products[h, d][:, u * P : (u + 1) * P],
+                    rhs=identity[:],
+                    is_transpose=True,
+                    start=(d == 0 and u == 0),
+                    stop=(d == turns - 1 and u == V // P - 1),
+                )
+
+        def turn_back(h, bank):
+            turned = keep.tile([P, V], F32, name=f"turned{h}")
+            nc.scalar.copy(turned[:], bank[:, 0:V])
+            back = psum.tile([P, T], F32, name=f"back{h}")
+            for u in range(V // P):
+                nc.tensor.transpose(back[:, u * P : (u + 1) * P], turned[:, u * P : (u + 1) * P], identity[:])
+            return back
+
+        sums = [psum.tile([P, T], F32, name=f"sums{h}") for h in range(HALVES)]
+        second = psum.tile([P, T], F32, name="second")
+        for d in range(D):
+            gather(0, d)
+            add_turned(sums[0], 0, d, D)
+            if 1 <= d <= PASSES:
+                c = d - 1
+                interleave(on_scalar, w_bf[1, c], w_raw[1, c], 0, 0, P)
+            if 2 <= d <= PASSES + 1:
+                c = d - 2
+                quantize(nc, w_codes[1, c], w_scales[1, c], w_bf[1, c], 0, P)
+            if d == PASSES + 1:
+                for c in range(PASSES):
+                    project(second, 1, c, 0, T)
+                nc.scalar.activation(y[1][:], second[:], RELU, bias=bias[:, 1:2])
+
+        back = turn_back(0, sums[0])
+        nc.scalar.copy(result[0][:], back[:, 0:V])
+        nc.sync.dma_start(out[0:P, :], result[0][:])
+
+        for d in range(D):
+            gather(1, d)
+            if d < D - TAIL_TURNS:
+                add_turned(sums[1], 1, d, D - TAIL_TURNS)
+        back = turn_back(1, sums[1])
+        partial = keep.tile([P, V], F32, name="partial")
+        for u in range(V // P):
+            cols = slice(u * P, (u + 1) * P)
+            nc.vector.tensor_tensor(partial[:, cols], products[1, D - 2][:, cols], back[:, cols], ADD)
+        for u in range(V // P):
+            cols = slice(u * P, (u + 1) * P)
+            nc.vector.tensor_tensor(result[1][:, cols], partial[:, cols], products[1, D - 1][:, cols], ADD)
+        nc.sync.dma_start(out[P : 2 * P, :], result[1][:])

@@ -23,12 +23,11 @@ K_PASS = P * PACK
 PASSES = K // K_PASS
 HALVES = N // P
 NODE_GROUPS = ((0, 256), (256, 384), (384, 512))
-TAIL_TURNS = 2
 
 
 def interleave(copy, grouped, raw, src0, dst0, width):
-    src = raw[:, :, src0 : src0 + width].rearrange("p j (c i) -> p c j i", i=4)
-    dst = grouped[:, dst0 : dst0 + width, :].rearrange("p (c i) j -> p c j i", i=4)
+    src = raw[:, :, src0 : src0 + width].rearrange("p j (c i) -> p c j i", i=2)
+    dst = grouped[:, dst0 : dst0 + width, :].rearrange("p (c i) j -> p c j i", i=2)
     copy(dst, src)
 
 
@@ -62,15 +61,14 @@ def tile_picked_agg_lin_relu_sub_l_kernel(
         x_codes = [keep.tile([P, T], U32, name=f"x_codes{c}", align_bytes=64) for c in range(PASSES)]
         x_scales = [keep.tile([P, T], U8, name=f"x_scales{c}", align_bytes=64) for c in range(PASSES)]
         hc = [(h, c) for h in range(HALVES) for c in range(PASSES)]
-        w_raw = {(h, c): keep.tile([P, PACK, P], F32, name=f"w_raw{h}{c}") for h, c in hc}
+        w_raw = {(h, c): keep.tile([P, PACK, P], F32, name=f"w_raw{h}{c}", tag=f"w_raw{h}{c}") for h, c in hc}
         w_bf = {(h, c): keep.tile([P, P, PACK], BF16, name=f"w_bf{h}{c}", align_bytes=64) for h, c in hc}
         w_codes = {(h, c): keep.tile([P, P], U32, name=f"w_codes{h}{c}", align_bytes=64) for h, c in hc}
         w_scales = {(h, c): keep.tile([P, P], U8, name=f"w_scales{h}{c}", align_bytes=64) for h, c in hc}
-        y = [keep.tile([P, T], F32, name=f"y{h}") for h in range(HALVES)]
         result = [keep.tile([P, V], F32, name=f"result{h}") for h in range(HALVES)]
 
         def load_x(c, t0, t1):
-            raw = keep.tile([P, PACK, t1 - t0], F32, name=f"x_raw{c}_{t0}")
+            raw = keep.tile([P, PACK, t1 - t0], F32, name=f"x_raw{c}_{t0}", tag=f"x_raw{c}_{t0}")
             rows = xT[c * K_PASS : (c + 1) * K_PASS, t0:t1]
             nc.sync.dma_start(raw[:], rows.rearrange("(p j) t -> p j t", j=PACK))
             return raw
@@ -112,16 +110,15 @@ def tile_picked_agg_lin_relu_sub_l_kernel(
         load_w(0, 0)
         x_raw[1] = load_x(1, 0, T)
         load_w(0, 1)
+        last = [load_x(2, *NODE_GROUPS[0])]
         load_w(0, 2)
-        last = [load_x(2, t0, t1) for t0, t1 in NODE_GROUPS]
+        last.extend(load_x(2, t0, t1) for t0, t1 in NODE_GROUPS[1:])
         load_list(0)
-        load_gate(0, 0, 1)
-        load_w(1, 0)
+        load_gate(0, 0, 3)
         load_list(1)
-        load_gate(0, 1, 3)
-        load_w(1, 1)
-        load_w(1, 2)
         load_list(2)
+        for c in range(PASSES):
+            load_w(1, c)
         load_list(3)
         load_gate(0, 3, 5)
         load_list(4)
@@ -144,28 +141,35 @@ def tile_picked_agg_lin_relu_sub_l_kernel(
                 project(bank, 0, c, t0, t1)
 
         c = PASSES - 1
-        interleave(on_scalar, w_bf[0, c], w_raw[0, c], 0, 0, P)
-        quantize(nc, w_codes[0, c], w_scales[0, c], w_bf[0, c], 0, P)
         interleave(on_scalar, x_bf[c], last[0], 0, 0, 128)
         interleave(on_vector, x_bf[c], last[0], 128, 128, 128)
-        interleave(on_vector, x_bf[c], last[1], 0, 256, 128)
+        interleave(on_scalar, w_bf[0, c], w_raw[0, c], 0, 0, P)
         quantize(nc, x_codes[c], x_scales[c], x_bf[c], 0, 256)
+        interleave(on_scalar, x_bf[c], last[1], 0, 256, 64)
+        interleave(on_vector, x_bf[c], last[1], 64, 320, 64)
+        quantize(nc, w_codes[0, c], w_scales[0, c], w_bf[0, c], 0, P)
         project(banks[0], 0, c, 0, 256)
-        interleave(on_scalar, x_bf[c], last[2], 0, 384, 64)
-        interleave(on_vector, x_bf[c], last[2], 64, 448, 64)
         quantize(nc, x_codes[c], x_scales[c], x_bf[c], 256, 384)
         project(banks[1], 0, c, 256, 384)
+        interleave(on_scalar, x_bf[c], last[2], 0, 384, 64)
+        interleave(on_vector, x_bf[c], last[2], 64, 448, 64)
         quantize(nc, x_codes[c], x_scales[c], x_bf[c], 384, 512)
         project(banks[2], 0, c, 384, 512)
-        nc.scalar.activation(y[0][:, 0:256], banks[0][:, 0:256], RELU, bias=bias[:, 0:1])
-        nc.scalar.activation(y[0][:, 256:384], banks[1][:, 0:128], RELU, bias=bias[:, 0:1])
+        y = [keep.tile([P, T], F32, name="y0", tag="x_raw2_384"), keep.tile([P, T], F32, name="y1")]
+        for bank, (t0, t1) in zip(banks[:2], NODE_GROUPS[:2]):
+            nc.scalar.activation(y[0][:, t0:t1], bank[:, 0 : t1 - t0], RELU, bias=bias[:, 0:1])
         nc.vector.tensor_scalar(y[0][:, 384:512], banks[2][:, 0:128], bias[:, 0:1], 0.0, ADD, MAX)
 
         products = {}
 
-        def gather(h, d):
-            products[h, d] = keep.tile([P, V], F32, name=f"product{h}_{d}")
-            nc.vector.tensor_tensor(products[h, d][:], y[h][:].indirect(offsets[d][:]), gates[h, d], MULT)
+        def gather(h, d, pieces):
+            tag = f"w_raw1{d - 1}" if h == 0 and 2 <= d <= PASSES else f"product{h}_{d}"
+            products[h, d] = keep.tile([P, V], F32, name=f"product{h}_{d}", tag=tag)
+            width = V // pieces
+            for v0 in range(0, V, width):
+                picked = y[h][:].indirect(offsets[d][:, v0 // 16 : (v0 + width) // 16])
+                cols = slice(v0, v0 + width)
+                nc.vector.tensor_tensor(products[h, d][:, cols], picked, gates[h, d][:, cols], MULT)
 
         def add_turned(bank, h, d, turns):
             for u in range(V // P):
@@ -189,33 +193,30 @@ def tile_picked_agg_lin_relu_sub_l_kernel(
         sums = [psum.tile([P, T], F32, name=f"sums{h}") for h in range(HALVES)]
         second = psum.tile([P, T], F32, name="second")
         for d in range(D):
-            gather(0, d)
-            add_turned(sums[0], 0, d, D)
             if 1 <= d <= PASSES:
                 c = d - 1
                 interleave(on_scalar, w_bf[1, c], w_raw[1, c], 0, 0, P)
-            if 2 <= d <= PASSES + 1:
-                c = d - 2
                 quantize(nc, w_codes[1, c], w_scales[1, c], w_bf[1, c], 0, P)
-            if d == PASSES + 1:
-                for c in range(PASSES):
-                    project(second, 1, c, 0, T)
+                project(second, 1, c, 0, T)
+            if d == PASSES:
                 nc.scalar.activation(y[1][:], second[:], RELU, bias=bias[:, 1:2])
-
+            gather(0, d, 1)
+            add_turned(sums[0], 0, d, D)
         back = turn_back(0, sums[0])
         nc.scalar.copy(result[0][:], back[:, 0:V])
         nc.sync.dma_start(out[0:P, :], result[0][:])
 
-        for d in range(D):
-            gather(1, d)
-            if d < D - TAIL_TURNS:
-                add_turned(sums[1], 1, d, D - TAIL_TURNS)
+        for d in range(D - 2):
+            gather(1, d, 1)
+            add_turned(sums[1], 1, d, D - 2)
         back = turn_back(1, sums[1])
-        partial = keep.tile([P, V], F32, name="partial")
+        gather(1, D - 2, 1)
+        gather(1, D - 1, 2)
+        pair = keep.tile([P, V], F32, name="pair")
         for u in range(V // P):
             cols = slice(u * P, (u + 1) * P)
-            nc.vector.tensor_tensor(partial[:, cols], products[1, D - 2][:, cols], back[:, cols], ADD)
+            nc.vector.tensor_tensor(pair[:, cols], products[1, D - 2][:, cols], products[1, D - 1][:, cols], ADD)
         for u in range(V // P):
             cols = slice(u * P, (u + 1) * P)
-            nc.vector.tensor_tensor(result[1][:, cols], partial[:, cols], products[1, D - 1][:, cols], ADD)
+            nc.vector.tensor_tensor(result[1][:, cols], pair[:, cols], back[:, cols], ADD)
         nc.sync.dma_start(out[P : 2 * P, :], result[1][:])

@@ -53,6 +53,7 @@ def tile_picked_agg_lin_relu_sub_l_kernel(
 
         offsets = [keep.tile([P, V // 16], U16, name=f"offsets{d}") for d in range(D)]
         bias = keep.tile([P, HALVES], F32, name="bias")
+        bias_rows = keep.tile([P, P], F32, name="bias_rows")
         identity = keep.tile([P, P], F32, name="identity")
         warm_in = keep.tile([P, 1], F32, name="warm_in")
         warm_out = keep.tile([P, 1], F32, name="warm_out")
@@ -99,11 +100,14 @@ def tile_picked_agg_lin_relu_sub_l_kernel(
                 stop=(c == PASSES - 1),
             )
 
-        with nc.allow_non_contiguous_dma(reason="one bias value a partition"):
-            nc.scalar.dma_start(bias[:], b.rearrange("(h p) o -> p (h o)", p=P))
+        nc.vector.memset(bias_rows[:], 0.0)
+        nc.scalar.dma_start(bias_rows[0:HALVES, :], b.rearrange("(h p) o -> h (p o)", p=P))
         nc.vector.memset(warm_in[:], 0.0)
         nc.scalar.activation(warm_out[:], warm_in[:], RELU)
         make_identity(nc, identity[:])
+        bias_turned = psum.tile([P, T], F32, name="bias_turned")
+        nc.tensor.transpose(bias_turned[:, 0:P], bias_rows[:], identity[:])
+        nc.scalar.copy(bias[:], bias_turned[:, 0:HALVES])
 
         x_raw = {}
         x_raw[0] = load_x(0, 0, T)
@@ -129,7 +133,7 @@ def tile_picked_agg_lin_relu_sub_l_kernel(
         load_gate(1, 0, 4)
         load_gate(1, 4, 8)
 
-        banks = [psum.tile([P, T], F32, name=f"bank{g}") for g in range(len(NODE_GROUPS))]
+        banks = [psum.tile([P, T], F32, name=f"bank{g}", tag=f"bank{g}") for g in range(len(NODE_GROUPS))]
         for c in range(PASSES - 1):
             interleave(on_scalar, x_bf[c], x_raw[c], 0, 0, 256)
             interleave(on_vector, x_bf[c], x_raw[c], 256, 256, 256)
@@ -190,7 +194,7 @@ def tile_picked_agg_lin_relu_sub_l_kernel(
                 nc.tensor.transpose(back[:, u * P : (u + 1) * P], turned[:, u * P : (u + 1) * P], identity[:])
             return back
 
-        sums = [psum.tile([P, T], F32, name=f"sums{h}") for h in range(HALVES)]
+        sums = [psum.tile([P, T], F32, name="sums0")]
         second = psum.tile([P, T], F32, name="second")
         for d in range(D):
             if 1 <= d <= PASSES:
@@ -206,17 +210,29 @@ def tile_picked_agg_lin_relu_sub_l_kernel(
         nc.scalar.copy(result[0][:], back[:, 0:V])
         nc.sync.dma_start(out[0:P, :], result[0][:])
 
+        blocks = [slice(u * P, (u + 1) * P) for u in range(V // P)]
+        block_sums = [psum.tile([P, T], F32, name=f"block_sum{u}", tag=f"bank{u}") for u in range(V // P)]
         for d in range(D - 2):
             gather(1, d, 1)
-            add_turned(sums[1], 1, d, D - 2)
-        back = turn_back(1, sums[1])
+            for bank, cols in zip(block_sums, blocks):
+                nc.tensor.matmul(
+                    bank[:, 0:P],
+                    lhsT=products[1, d][:, cols],
+                    rhs=identity[:],
+                    is_transpose=True,
+                    start=(d == 0),
+                    stop=(d == D - 3),
+                )
+        turned = keep.tile([P, V], F32, name="turned1")
+        backs = [psum.tile([P, T], F32, name="back1a"), psum.tile([P, T], F32, name="back1b", tag="bank2")]
+        for bank, back, cols in zip(block_sums, backs, blocks):
+            nc.scalar.copy(turned[:, cols], bank[:, 0:P])
+            nc.tensor.transpose(back[:, 0:P], turned[:, cols], identity[:])
         gather(1, D - 2, 1)
         gather(1, D - 1, 2)
         pair = keep.tile([P, V], F32, name="pair")
-        for u in range(V // P):
-            cols = slice(u * P, (u + 1) * P)
+        for cols in blocks:
             nc.vector.tensor_tensor(pair[:, cols], products[1, D - 2][:, cols], products[1, D - 1][:, cols], ADD)
-        for u in range(V // P):
-            cols = slice(u * P, (u + 1) * P)
-            nc.vector.tensor_tensor(result[1][:, cols], pair[:, cols], back[:, cols], ADD)
-        nc.sync.dma_start(out[P : 2 * P, :], result[1][:])
+        for back, cols in zip(backs, blocks):
+            nc.vector.tensor_tensor(result[1][:, cols], pair[:, cols], back[:, 0:P], ADD)
+            nc.sync.dma_start(out[P : 2 * P, cols], result[1][:, cols])

@@ -117,12 +117,14 @@ def tile_picked_agg_lin_relu_sub_l_kernel(
         last = [load_x(2, *NODE_GROUPS[0])]
         load_w(0, 2)
         last.extend(load_x(2, t0, t1) for t0, t1 in NODE_GROUPS[1:])
+        load_w(1, 0)
         load_list(0)
-        load_gate(0, 0, 3)
+        load_gate(0, 0, 2)
         load_list(1)
+        load_w(1, 1)
         load_list(2)
-        for c in range(PASSES):
-            load_w(1, c)
+        load_gate(0, 2, 3)
+        load_w(1, 2)
         load_list(3)
         load_gate(0, 3, 5)
         load_list(4)
@@ -162,7 +164,11 @@ def tile_picked_agg_lin_relu_sub_l_kernel(
         y = [keep.tile([P, T], F32, name="y0", tag="x_raw2_384"), keep.tile([P, T], F32, name="y1")]
         for bank, (t0, t1) in zip(banks[:2], NODE_GROUPS[:2]):
             nc.scalar.activation(y[0][:, t0:t1], bank[:, 0 : t1 - t0], RELU, bias=bias[:, 0:1])
+        interleave(on_scalar, w_bf[1, 0], w_raw[1, 0], 0, 0, P)
         nc.vector.tensor_scalar(y[0][:, 384:512], banks[2][:, 0:128], bias[:, 0:1], 0.0, ADD, MAX)
+        quantize(nc, w_codes[1, 0], w_scales[1, 0], w_bf[1, 0], 0, P)
+        second = psum.tile([P, T], F32, name="second")
+        project(second, 1, 0, 0, T)
 
         products = {}
 
@@ -195,9 +201,8 @@ def tile_picked_agg_lin_relu_sub_l_kernel(
             return back
 
         sums = [psum.tile([P, T], F32, name="sums0")]
-        second = psum.tile([P, T], F32, name="second")
         for d in range(D):
-            if 1 <= d <= PASSES:
+            if 2 <= d <= PASSES:
                 c = d - 1
                 interleave(on_scalar, w_bf[1, c], w_raw[1, c], 0, 0, P)
                 quantize(nc, w_codes[1, c], w_scales[1, c], w_bf[1, c], 0, P)

from contextlib import ExitStack

import concourse.mybir as mybir
from concourse.masks import make_identity

K, T, D, V, N = 1536, 512, 8, 256, 256
FLOPS = 2 * K * T * N + 2 * D * V * N

F32 = mybir.dt.float32
BF16 = mybir.dt.bfloat16
U32 = mybir.dt.uint32
U16 = mybir.dt.uint16
U8 = mybir.dt.uint8
FP8X4 = mybir.dt.float8_e4m3fn_x4
ADD = mybir.AluOpType.add
MULT = mybir.AluOpType.mult
MAX = mybir.AluOpType.max
RELU = mybir.ActivationFunctionType.Relu

P = 128
PACK = 4
K_PASS = P * PACK
PASSES = K // K_PASS
HALVES = N // P
NODE_GROUPS = ((0, 256), (256, 384), (384, 512))


def interleave(copy, grouped, raw, src0, dst0, width):
    src = raw[:, :, src0 : src0 + width].rearrange("p j (c i) -> p c j i", i=2)
    dst = grouped[:, dst0 : dst0 + width, :].rearrange("p (c i) j -> p c j i", i=2)
    copy(dst, src)


def quantize(nc, codes, scales, grouped, c0, c1):
    nc.vector.quantize_mx(
        out=codes[:, c0:c1].bitcast(FP8X4),
        scales=scales[:, c0:c1],
        in_=grouped[:, c0:c1, :].rearrange("p w j -> p (w j)"),
    )


def tile_picked_agg_lin_relu_sub_l_kernel(
    tc, xT, w, b, gate, pos1, pos2, pos3, pos4, pos5, pos6, pos7, pos8, out
):
    nc = tc.nc
    lists = (pos1, pos2, pos3, pos4, pos5, pos6, pos7, pos8)
    on_vector = nc.vector.tensor_copy
    on_scalar = nc.scalar.copy

    with ExitStack() as ctx:
        keep = ctx.enter_context(tc.tile_pool(name="keep", bufs=1))
        psum = ctx.enter_context(tc.psum_pool(name="psum", bufs=1))

        offsets = [keep.tile([P, V // 16], U16, name=f"offsets{d}") for d in range(D)]
        bias = keep.tile([P, HALVES], F32, name="bias")
        bias_rows = keep.tile([P, P], F32, name="bias_rows")
        identity = keep.tile([P, P], F32, name="identity")
        warm_in = keep.tile([P, 1], F32, name="warm_in")
        warm_out = keep.tile([P, 1], F32, name="warm_out")

        x_bf = [keep.tile([P, T, PACK], BF16, name=f"x_bf{c}", align_bytes=64) for c in range(PASSES)]
        x_codes = [keep.tile([P, T], U32, name=f"x_codes{c}", align_bytes=64) for c in range(PASSES)]
        x_scales = [keep.tile([P, T], U8, name=f"x_scales{c}", align_bytes=64) for c in range(PASSES)]
        hc = [(h, c) for h in range(HALVES) for c in range(PASSES)]
        w_raw = {(h, c): keep.tile([P, PACK, P], F32, name=f"w_raw{h}{c}", tag=f"w_raw{h}{c}") for h, c in hc}
        w_bf = {(h, c): keep.tile([P, P, PACK], BF16, name=f"w_bf{h}{c}", align_bytes=64) for h, c in hc}
        w_codes = {(h, c): keep.tile([P, P], U32, name=f"w_codes{h}{c}", align_bytes=64) for h, c in hc}
        w_scales = {(h, c): keep.tile([P, P], U8, name=f"w_scales{h}{c}", align_bytes=64) for h, c in hc}
        result = [keep.tile([P, V], F32, name=f"result{h}") for h in range(HALVES)]

        def load_x(c, t0, t1):
            raw = keep.tile([P, PACK, t1 - t0], F32, name=f"x_raw{c}_{t0}", tag=f"x_raw{c}_{t0}")
            rows = xT[c * K_PASS : (c + 1) * K_PASS, t0:t1]
            nc.sync.dma_start(raw[:], rows.rearrange("(p j) t -> p j t", j=PACK))
            return raw

        def load_w(h, c):
            rows = w[c * K_PASS : (c + 1) * K_PASS, h * P : (h + 1) * P]
            nc.sync.dma_start(w_raw[h, c][:], rows.rearrange("(p j) m -> p j m", j=PACK))

        gates = {}

        def load_gate(h, d0, d1):
            tile = keep.tile([P, d1 - d0, V], F32, name=f"gate{h}_{d0}")
            nc.sync.dma_start(tile[:], gate[d0:d1, h * P : (h + 1) * P, :].rearrange("d m v -> m d v"))
            for d in range(d0, d1):
                gates[h, d] = tile[:, d - d0, :]

        def load_list(d):
            nc.sync.dma_start(offsets[d][:], lists[d])

        def project(bank, h, c, t0, t1):
            nc.tensor.matmul_mx(
                out=bank[:, 0 : t1 - t0],
                lhsT=w_codes[h, c][:].bitcast(FP8X4),
                lhsT_scale=w_scales[h, c][:],
                rhs=x_codes[c][:, t0:t1].bitcast(FP8X4),
                rhs_scale=x_scales[c][:, t0:t1],
                start=(c == 0),
                stop=(c == PASSES - 1),
            )

        nc.vector.memset(bias_rows[:], 0.0)
        nc.scalar.dma_start(bias_rows[0:HALVES, :], b.rearrange("(h p) o -> h (p o)", p=P))
        nc.vector.memset(warm_in[:], 0.0)
        nc.scalar.activation(warm_out[:], warm_in[:], RELU)
        make_identity(nc, identity[:])
        bias_turned = psum.tile([P, T], F32, name="bias_turned")
        nc.tensor.transpose(bias_turned[:, 0:P], bias_rows[:], identity[:])
        nc.scalar.copy(bias[:], bias_turned[:, 0:HALVES])

        x_raw = {}
        x_raw[0] = load_x(0, 0, T)
        load_w(0, 0)
        x_raw[1] = load_x(1, 0, T)
        load_w(0, 1)
        last = [load_x(2, *NODE_GROUPS[0])]
        load_w(0, 2)
        last.extend(load_x(2, t0, t1) for t0, t1 in NODE_GROUPS[1:])
        load_w(1, 0)
        load_list(0)
        load_gate(0, 0, 2)
        load_list(1)
        load_w(1, 1)
        load_list(2)
        load_gate(0, 2, 3)
        load_w(1, 2)
        load_list(3)
        load_gate(0, 3, 5)
        load_list(4)
        load_list(5)
        load_gate(0, 5, 8)
        load_list(6)
        load_list(7)
        load_gate(1, 0, 4)
        load_gate(1, 4, 8)

        banks = [psum.tile([P, T], F32, name=f"bank{g}", tag=f"bank{g}") for g in range(len(NODE_GROUPS))]
        for c in range(PASSES - 1):
            interleave(on_scalar, x_bf[c], x_raw[c], 0, 0, 256)
            interleave(on_vector, x_bf[c], x_raw[c], 256, 256, 256)
            interleave(on_scalar, w_bf[0, c], w_raw[0, c], 0, 0, P)
            quantize(nc, x_codes[c], x_scales[c], x_bf[c], 256, 512)
            quantize(nc, x_codes[c], x_scales[c], x_bf[c], 0, 256)
            quantize(nc, w_codes[0, c], w_scales[0, c], w_bf[0, c], 0, P)
            for bank, (t0, t1) in zip(banks, NODE_GROUPS):
                project(bank, 0, c, t0, t1)

        c = PASSES - 1
        interleave(on_scalar, x_bf[c], last[0], 0, 0, 128)
        interleave(on_vector, x_bf[c], last[0], 128, 128, 128)
        interleave(on_scalar, w_bf[0, c], w_raw[0, c], 0, 0, P)
        quantize(nc, x_codes[c], x_scales[c], x_bf[c], 0, 256)
        interleave(on_scalar, x_bf[c], last[1], 0, 256, 64)
        interleave(on_vector, x_bf[c], last[1], 64, 320, 64)
        quantize(nc, w_codes[0, c], w_scales[0, c], w_bf[0, c], 0, P)
        project(banks[0], 0, c, 0, 256)
        quantize(nc, x_codes[c], x_scales[c], x_bf[c], 256, 384)
        project(banks[1], 0, c, 256, 384)
        interleave(on_scalar, x_bf[c], last[2], 0, 384, 64)
        interleave(on_vector, x_bf[c], last[2], 64, 448, 64)
        quantize(nc, x_codes[c], x_scales[c], x_bf[c], 384, 512)
        project(banks[2], 0, c, 384, 512)
        y = [keep.tile([P, T], F32, name="y0", tag="x_raw2_384"), keep.tile([P, T], F32, name="y1")]
        for bank, (t0, t1) in zip(banks[:2], NODE_GROUPS[:2]):
            nc.scalar.activation(y[0][:, t0:t1], bank[:, 0 : t1 - t0], RELU, bias=bias[:, 0:1])
        interleave(on_scalar, w_bf[1, 0], w_raw[1, 0], 0, 0, P)
        nc.vector.tensor_scalar(y[0][:, 384:512], banks[2][:, 0:128], bias[:, 0:1], 0.0, ADD, MAX)
        quantize(nc, w_codes[1, 0], w_scales[1, 0], w_bf[1, 0], 0, P)
        second = psum.tile([P, T], F32, name="second")
        project(second, 1, 0, 0, T)

        products = {}

        def gather(h, d, pieces):
            tag = f"w_raw1{d - 1}" if h == 0 and 2 <= d <= PASSES else f"product{h}_{d}"
            products[h, d] = keep.tile([P, V], F32, name=f"product{h}_{d}", tag=tag)
            width = V // pieces
            for v0 in range(0, V, width):
                picked = y[h][:].indirect(offsets[d][:, v0 // 16 : (v0 + width) // 16])
                cols = slice(v0, v0 + width)
                nc.vector.tensor_tensor(products[h, d][:, cols], picked, gates[h, d][:, cols], MULT)

        def add_turned(bank, h, d, turns):
            for u in range(V // P):
                nc.tensor.matmul(
                    bank[:, u * P : (u + 1) * P],
                    lhsT=products[h, d][:, u * P : (u + 1) * P],
                    rhs=identity[:],
                    is_transpose=True,
                    start=(d == 0 and u == 0),
                    stop=(d == turns - 1 and u == V // P - 1),
                )

        def turn_back(h, bank):
            turned = keep.tile([P, V], F32, name=f"turned{h}")
            nc.scalar.copy(turned[:], bank[:, 0:V])
            back = psum.tile([P, T], F32, name=f"back{h}")
            for u in range(V // P):
                nc.tensor.transpose(back[:, u * P : (u + 1) * P], turned[:, u * P : (u + 1) * P], identity[:])
            return back

        sums = [psum.tile([P, T], F32, name="sums0")]
        for d in range(D):
            if 2 <= d <= PASSES:
                c = d - 1
                interleave(on_scalar, w_bf[1, c], w_raw[1, c], 0, 0, P)
                quantize(nc, w_codes[1, c], w_scales[1, c], w_bf[1, c], 0, P)
                project(second, 1, c, 0, T)
            if d == PASSES:
                nc.scalar.activation(y[1][:], second[:], RELU, bias=bias[:, 1:2])
            gather(0, d, 1)
            add_turned(sums[0], 0, d, D)
        back = turn_back(0, sums[0])
        nc.scalar.copy(result[0][:], back[:, 0:V])
        nc.sync.dma_start(out[0:P, :], result[0][:])

        blocks = [slice(u * P, (u + 1) * P) for u in range(V // P)]
        block_sums = [psum.tile([P, T], F32, name=f"block_sum{u}", tag=f"bank{u}") for u in range(V // P)]
        for d in range(D - 2):
            gather(1, d, 1)
            for bank, cols in zip(block_sums, blocks):
                nc.tensor.matmul(
                    bank[:, 0:P],
                    lhsT=products[1, d][:, cols],
                    rhs=identity[:],
                    is_transpose=True,
                    start=(d == 0),
                    stop=(d == D - 3),
                )
        turned = keep.tile([P, V], F32, name="turned1")
        backs = [psum.tile([P, T], F32, name="back1a"), psum.tile([P, T], F32, name="back1b", tag="bank2")]
        for bank, back, cols in zip(block_sums, backs, blocks):
            nc.scalar.copy(turned[:, cols], bank[:, 0:P])
            nc.tensor.transpose(back[:, 0:P], turned[:, cols], identity[:])
        gather(1, D - 2, 1)
        gather(1, D - 1, 2)
        pair = keep.tile([P, V], F32, name="pair")
        for cols in blocks:
            nc.vector.tensor_tensor(pair[:, cols], products[1, D - 2][:, cols], products[1, D - 1][:, cols], ADD)
        for back, cols in zip(backs, blocks):
            nc.vector.tensor_tensor(result[1][:, cols], pair[:, cols], back[:, 0:P], ADD)
            nc.sync.dma_start(out[P : 2 * P, cols], result[1][:, cols])
